import numpy as np
import ml_dtypes

BF16 = ml_dtypes.bfloat16


def bf(x):
    return np.asarray(x, np.float32).astype(BF16)


def f32(x):
    return np.asarray(x, np.float32)


def f64(x):
    return np.asarray(x).astype(np.float64)


def striped(idx):
    return np.tile(idx.reshape(-1, 16).T, (8, 1))


def rows(idx, k):
    return np.tile(idx, (k, 1))


def look(tab, idx):
    return np.take_along_axis(f64(tab), rows(idx, len(tab)), axis=1)


K, S, V, N, M = 128, 2048, 2048, 2048, 512


def setup_inputs():
    return {"tab": f32(np.random.standard_normal((K, S))), "s": f32(np.random.uniform(0.5, 1.5, (K, 1))), "c": f32(0.3 * np.random.standard_normal((K, 1))), "w": bf(np.random.standard_normal((K, M)) / np.sqrt(K)), "b": f32(0.5 * np.random.standard_normal((M, 1))), "offs": striped(np.random.randint(0, S, N))}


def reference(tab, s, c, w, b, offs):
    idx = offs[:16].T.reshape(-1)
    t = look(tab, idx)
    x = f64(s) * t + f64(c)
    y = f64(w).T @ x
    return y + f64(b)

@@ -1,0 +1,60 @@
+import concourse.mybir as mybir
+
+F32, BF16, U16 = mybir.dt.float32, mybir.dt.bfloat16, mybir.dt.uint16
+MULT, ADD = mybir.AluOpType.mult, mybir.AluOpType.add
+IDENTITY = mybir.ActivationFunctionType.Identity
+
+P = 128
+S = 2048
+N = 2048
+M = 512
+BLOCKS = M // P
+PIECE = 512
+PIECES = N // PIECE
+LIST_COLUMNS = PIECE // 16
+
+FLOPS = 2 * P * M * N
+
+
+def tile_lookup_deq_affp_bias_kernel(tc, tab, s, c, w, b, offs, out):
+    nc = tc.nc
+    with (
+        tc.tile_pool(name="held", bufs=1) as held,
+        tc.tile_pool(name="columns", bufs=2) as columns,
+        tc.tile_pool(name="results", bufs=8) as results,
+        tc.psum_pool(name="products", bufs=8) as products,
+    ):
+        table = held.tile([P, S], F32)
+        nc.scalar.dma_start(table[:], tab)
+        offsets = held.tile([P, N // 16], U16)
+        nc.sync.dma_start(offsets[:], offs)
+        scale = held.tile([P, 1], F32)
+        nc.sync.dma_start(scale[:], s)
+        shift = held.tile([P, 1], F32)
+        nc.sync.dma_start(shift[:], c)
+        weights = held.tile([P, M], BF16)
+        nc.sync.dma_start(weights[:], w)
+        bias = held.tile([P, BLOCKS], F32)
+        with nc.allow_non_contiguous_dma(reason="512 biases, one element each"):
+            nc.sync.dma_start(bias[:], b.rearrange("(q p) o -> p (q o)", p=P))
+
+        for piece in range(PIECES):
+            listed = offsets[:, piece * LIST_COLUMNS : (piece + 1) * LIST_COLUMNS]
+            affine = columns.tile([P, PIECE], F32)
+            nc.vector.tensor_scalar(
+                affine[:], table[:].indirect(listed), scale[:], shift[:], op0=MULT, op1=ADD
+            )
+            x = columns.tile([P, PIECE], BF16)
+            nc.vector.tensor_copy(x[:], affine[:])
+            for block in range(BLOCKS):
+                product = products.tile([P, PIECE], F32)
+                nc.tensor.matmul(
+                    product[:], weights[:, block * P : (block + 1) * P], x[:], start=True, stop=True
+                )
+                result = results.tile([P, PIECE], F32)
+                nc.scalar.activation(
+                    result[:], product[:], IDENTITY, bias=bias[:, block : block + 1], scale=1.0
+                )
+                nc.sync.dma_start(
+                    out[block * P : (block + 1) * P, piece * PIECE : (piece + 1) * PIECE], result[:]
+                )

@@ -9,9 +9,9 @@ S = 2048
 N = 2048
 M = 512
 BLOCKS = M // P
-PIECE = 512
-PIECES = N // PIECE
-LIST_COLUMNS = PIECE // 16
+BANK = 512
+WIDTHS = (256, 256, 512, 512, 512)
+VECTOR_HELPS_FROM = BANK
 
 FLOPS = 2 * P * M * N
 
@@ -20,8 +20,7 @@ def tile_lookup_deq_affp_bias_kernel(tc, tab, s, c, w, b, offs, out):
     nc = tc.nc
     with (
         tc.tile_pool(name="held", bufs=1) as held,
-        tc.tile_pool(name="columns", bufs=2) as columns,
-        tc.tile_pool(name="results", bufs=8) as results,
+        tc.tile_pool(name="looked_up", bufs=2) as looked_up,
         tc.psum_pool(name="products", bufs=8) as products,
     ):
         table = held.tile([P, S], F32)
@@ -32,29 +31,38 @@ def tile_lookup_deq_affp_bias_kernel(tc, tab, s, c, w, b, offs, out):
         nc.sync.dma_start(scale[:], s)
         shift = held.tile([P, 1], F32)
         nc.sync.dma_start(shift[:], c)
-        weights = held.tile([P, M], BF16)
-        nc.sync.dma_start(weights[:], w)
         bias = held.tile([P, BLOCKS], F32)
-        with nc.allow_non_contiguous_dma(reason="512 biases, one element each"):
-            nc.sync.dma_start(bias[:], b.rearrange("(q p) o -> p (q o)", p=P))
+        nc.sync.dma_start(bias[:], b.rearrange("(p q) o -> p (q o)", q=BLOCKS))
+        weights = held.tile([P, M], BF16)
+        nc.scalar.dma_start(weights[:], w)
+        block_weights = weights[:].rearrange("r (p q) -> r q p", q=BLOCKS)
+        block_rows = out.rearrange("(p q) n -> q p n", q=BLOCKS)
 
-        for piece in range(PIECES):
-            listed = offsets[:, piece * LIST_COLUMNS : (piece + 1) * LIST_COLUMNS]
-            affine = columns.tile([P, PIECE], F32)
+        starts = [sum(WIDTHS[:i]) for i in range(len(WIDTHS))]
+
+        columns = []
+        for start, width in zip(starts, WIDTHS):
+            listed = offsets[:, start // 16 : (start + width) // 16]
+            affine = looked_up.tile([P, width], F32, name="affine")
             nc.vector.tensor_scalar(
                 affine[:], table[:].indirect(listed), scale[:], shift[:], op0=MULT, op1=ADD
             )
-            x = columns.tile([P, PIECE], BF16)
-            nc.vector.tensor_copy(x[:], affine[:])
+            x = held.tile([P, width], BF16, name="x_%d" % start)
+            nc.gpsimd.tensor_copy(x[:], affine[:])
+            columns.append(x)
+
+        for start, width, x in zip(starts, WIDTHS, columns):
             for block in range(BLOCKS):
-                product = products.tile([P, PIECE], F32)
+                product = products.tile([P, BANK], F32)
                 nc.tensor.matmul(
-                    product[:], weights[:, block * P : (block + 1) * P], x[:], start=True, stop=True
+                    product[:, :width], block_weights[:, block, :], x[:], start=True, stop=True
                 )
-                result = results.tile([P, PIECE], F32)
-                nc.scalar.activation(
-                    result[:], product[:], IDENTITY, bias=bias[:, block : block + 1], scale=1.0
-                )
-                nc.sync.dma_start(
-                    out[block * P : (block + 1) * P, piece * PIECE : (piece + 1) * PIECE], result[:]
-                )
+                result = held.tile([P, width], F32, name="result_%d_%d" % (start, block))
+                block_bias = bias[:, block : block + 1]
+                if start >= VECTOR_HELPS_FROM and block % 2 == 1:
+                    nc.vector.tensor_scalar(result[:], product[:, :width], block_bias, None, op0=ADD)
+                else:
+                    nc.scalar.activation(
+                        result[:], product[:, :width], IDENTITY, bias=block_bias, scale=1.0
+                    )
+                nc.sync.dma_start(block_rows[block, :, start : start + width], result[:])

@@ -12,6 +12,7 @@ BLOCKS = M // P
 BANK = 512
 WIDTHS = (256, 256, 512, 512, 512)
 VECTOR_HELPS_FROM = BANK
+WARM_UP = 12
 
 FLOPS = 2 * P * M * N
 
@@ -37,6 +38,14 @@ def tile_lookup_deq_affp_bias_kernel(tc, tab, s, c, w, b, offs, out):
         nc.scalar.dma_start(weights[:], w)
         block_weights = weights[:].rearrange("r (p q) -> r q p", q=BLOCKS)
         block_rows = out.rearrange("(p q) n -> q p n", q=BLOCKS)
+
+        zeros = held.tile([P, BANK], BF16)
+        nc.gpsimd.memset(zeros[:], 0.0)
+        warm = held.tile([P, 1], F32)
+        nc.scalar.activation(warm[:], zeros[:, :1], IDENTITY, bias=0.0, scale=1.0)
+        for repeat in range(WARM_UP):
+            product = products.tile([P, BANK], F32)
+            nc.tensor.matmul(product[:], zeros[:, :P], zeros[:], start=True, stop=True)
 
         starts = [sum(WIDTHS[:i]) for i in range(len(WIDTHS))]
 

import concourse.mybir as mybir

F32, BF16, U16 = mybir.dt.float32, mybir.dt.bfloat16, mybir.dt.uint16
MULT, ADD = mybir.AluOpType.mult, mybir.AluOpType.add
IDENTITY = mybir.ActivationFunctionType.Identity

P = 128
S = 2048
N = 2048
M = 512
BLOCKS = M // P
BANK = 512
WIDTHS = (256, 256, 512, 512, 512)
VECTOR_HELPS_FROM = BANK
WARM_UP = 12

FLOPS = 2 * P * M * N


def tile_lookup_deq_affp_bias_kernel(tc, tab, s, c, w, b, offs, out):
    nc = tc.nc
    with (
        tc.tile_pool(name="held", bufs=1) as held,
        tc.tile_pool(name="looked_up", bufs=2) as looked_up,
        tc.psum_pool(name="products", bufs=8) as products,
    ):
        table = held.tile([P, S], F32)
        nc.scalar.dma_start(table[:], tab)
        offsets = held.tile([P, N // 16], U16)
        nc.sync.dma_start(offsets[:], offs)
        scale = held.tile([P, 1], F32)
        nc.sync.dma_start(scale[:], s)
        shift = held.tile([P, 1], F32)
        nc.sync.dma_start(shift[:], c)
        bias = held.tile([P, BLOCKS], F32)
        nc.sync.dma_start(bias[:], b.rearrange("(p q) o -> p (q o)", q=BLOCKS))
        weights = held.tile([P, M], BF16)
        nc.scalar.dma_start(weights[:], w)
        block_weights = weights[:].rearrange("r (p q) -> r q p", q=BLOCKS)
        block_rows = out.rearrange("(p q) n -> q p n", q=BLOCKS)

        zeros = held.tile([P, BANK], BF16)
        nc.gpsimd.memset(zeros[:], 0.0)
        warm = held.tile([P, 1], F32)
        nc.scalar.activation(warm[:], zeros[:, :1], IDENTITY, bias=0.0, scale=1.0)
        for repeat in range(WARM_UP):
            product = products.tile([P, BANK], F32)
            nc.tensor.matmul(product[:], zeros[:, :P], zeros[:], start=True, stop=True)

        starts = [sum(WIDTHS[:i]) for i in range(len(WIDTHS))]

        columns = []
        for start, width in zip(starts, WIDTHS):
            listed = offsets[:, start // 16 : (start + width) // 16]
            affine = looked_up.tile([P, width], F32, name="affine")
            nc.vector.tensor_scalar(
                affine[:], table[:].indirect(listed), scale[:], shift[:], op0=MULT, op1=ADD
            )
            x = held.tile([P, width], BF16, name="x_%d" % start)
            nc.gpsimd.tensor_copy(x[:], affine[:])
            columns.append(x)

        for start, width, x in zip(starts, WIDTHS, columns):
            for block in range(BLOCKS):
                product = products.tile([P, BANK], F32)
                nc.tensor.matmul(
                    product[:, :width], block_weights[:, block, :], x[:], start=True, stop=True
                )
                result = held.tile([P, width], F32, name="result_%d_%d" % (start, block))
                block_bias = bias[:, block : block + 1]
                if start >= VECTOR_HELPS_FROM and block % 2 == 1:
                    nc.vector.tensor_scalar(result[:], product[:, :width], block_bias, None, op0=ADD)
                else:
                    nc.scalar.activation(
                        result[:], product[:, :width], IDENTITY, bias=block_bias, scale=1.0
                    )
                nc.sync.dma_start(block_rows[block, :, start : start + width], result[:])
